import numpy as np
import ml_dtypes


def mxq(x, axis, fmt="e4m3"):
    dtype, down = {"e4m3": (ml_dtypes.float8_e4m3fn, 7), "e5m2": (ml_dtypes.float8_e5m2, 14)}[fmt]
    v = np.moveaxis(np.asarray(x, np.float32).astype(ml_dtypes.bfloat16).astype(np.float64), axis, -1)
    blocks = v.reshape(v.shape[:-1] + (-1, 32))
    amax = np.abs(blocks).max(-1, keepdims=True)
    byte = np.maximum(np.where(amax > 0, np.frexp(amax)[1] - 1 + 127, 0) - down, 1)
    scale = np.exp2(byte - 127.0)
    codes = (blocks / scale).astype(np.float32).astype(dtype).astype(np.float64)
    return np.moveaxis((codes * scale).reshape(v.shape), -1, axis)


WIDE = False


def mx_kscale(k):
    if not WIDE:
        return np.ones(k)
    levels = np.array([10, -10, 5, -5, 0])
    if k % 512:
        return np.exp2(np.random.permutation(np.resize(levels, k // 32))).repeat(32)
    a = np.empty((k // 512, 16))
    for p in range(k // 512):
        a[p, :8] = np.random.permutation(np.resize(levels, 8))
        for g in range(8):
            far = levels[np.abs(levels - a[p, g]) >= 10]
            a[p, g + 8] = far[np.random.randint(len(far))]
    return np.exp2(a.ravel()).repeat(32)


BF16 = ml_dtypes.bfloat16


def bf(x):
    return np.asarray(x, np.float32).astype(BF16)


def f64(x):
    return np.asarray(x).astype(np.float64)


E2M1 = np.array([0.0, 0.5, 1.0, 1.5, 2.0, 3.0, 4.0, 6.0, -0.0, -0.5, -1.0, -1.5, -2.0, -3.0, -4.0, -6.0])


def pack_weight(w, fmt):
    k, n = w.shape
    w = f64(bf(w)).reshape(k // 32, 32, n)
    amax = np.abs(w).max(1)
    if fmt == "e4m3":
        byte = np.frexp(amax)[1] - 1 + 127 - 7
    else:
        mant, ex = np.frexp(amax / 6.0)
        byte = np.where(mant > 0.5, ex, ex - 1) + 127
    byte = np.clip(np.where(amax > 0, byte, 1), 1, 254)
    scaled = (w * np.exp2(127.0 - byte)[:, None, :]).reshape(k, n).astype(np.float32)
    by_word = np.ascontiguousarray(scaled.reshape(k // 512, 128, 4, n).transpose(0, 1, 3, 2))
    if fmt == "e4m3":
        words = by_word.astype(ml_dtypes.float8_e4m3fn).view(np.uint8)
    else:
        c = by_word.astype(ml_dtypes.float4_e2m1fn).view(np.uint8) & 0xF
        words = c[..., 0::2] | (c[..., 1::2] << 4)
    return np.ascontiguousarray(words), np.ascontiguousarray(byte.astype(np.uint8).reshape(k // 512, 16, n))


def unpack_weight(words, scales, fmt):
    g, p, n, _ = words.shape
    if fmt == "e4m3":
        vals = np.ascontiguousarray(words).view(ml_dtypes.float8_e4m3fn).astype(np.float64)
    else:
        nib = np.empty((g, p, n, 4), np.uint8)
        nib[..., 0::2] = words & 0xF
        nib[..., 1::2] = words >> 4
        vals = E2M1[nib]
    vals = vals * np.repeat(np.exp2(scales.astype(np.float64) - 127.0), 8, axis=1)[..., None]
    return vals.transpose(0, 1, 3, 2).reshape(g * 512, n)
def pack4(w):
    words, scales = pack_weight(w, "e2m1")
    return words.reshape(words.shape[0], 128, -1), scales


def unpack4(words, scales):
    return unpack_weight(words.reshape(words.shape[0], 128, -1, 2), scales, "e2m1")


def planes(Y):
    n, m = Y.shape
    b = f64(bf(Y)).reshape(n // 32, 32, m)
    amax = np.abs(b).max(1)
    byte = np.clip(np.where(amax > 0, np.frexp(amax)[1] - 1 + 127 - 7, 1), 1, 254)
    codes = (b * np.exp2(127.0 - byte)[:, None, :]).reshape(n, m).astype(np.float32).astype(ml_dtypes.float8_e4m3fn).view(np.uint8)
    words = codes.reshape(n // 512, 128, 4, m).transpose(0, 1, 3, 2)
    return np.ascontiguousarray(words), np.ascontiguousarray(byte.astype(np.uint8).reshape(n // 512, 16, m))


M, K, N = 1024, 1536, 1024


def setup_inputs():
    rnd = np.random.standard_normal
    s = mx_kscale(K)
    t = mx_kscale(K)
    w_words, w_scales = pack4(rnd((K, N)) / np.sqrt(K) / t[:, None])
    return {
        "z": bf(0.7 * rnd((M, K))),
        "zdot": bf(1.2 * rnd((M, K)) * (t / s)[None, :]),
        "gain": bf((1 + 0.1 * rnd(K)) * s),
        "v": bf(1.3 * rnd((K, N)) / np.sqrt(K) / s[:, None]),
        "w_words": w_words,
        "w_scales": w_scales,
        "vb": bf(0.4 * rnd(N)),
        "rate": bf(np.exp(0.5 * rnd((M, N)))),
        "omega": bf(np.exp(0.8 * rnd(M))),
    }

def reference(z, zdot, gain, v, w_words, w_scales, vb, rate, omega):
    th = np.tanh(f64(z))
    H = f64(gain) * th
    Hdot = f64(gain) * (1 - th * th) * f64(zdot)
    W = unpack4(w_words, w_scales)
    direct = mxq(H, 1, "e4m3") @ mxq(f64(v), 0, "e4m3")
    through = mxq(Hdot, 1, "e4m3") @ W
    jv = direct + through + f64(vb)
    y = f64(omega)[:, None] * (f64(rate) * jv)
    Y = y
    words, scales = planes(Y)
    return y, words, scales

@@ -1,0 +1,345 @@
+from contextlib import ExitStack
+
+import concourse.mybir as mybir
+from concourse.masks import make_identity
+
+M, K, N = 1024, 1536, 1024
+FLOPS = 2 * 2 * M * K * N
+
+F32 = mybir.dt.float32
+BF16 = mybir.dt.bfloat16
+I32 = mybir.dt.int32
+U32 = mybir.dt.uint32
+U8 = mybir.dt.uint8
+FP8X4 = mybir.dt.float8_e4m3fn_x4
+FP4X4 = mybir.dt.float4_e2m1fn_x4
+ACT = mybir.ActivationFunctionType
+ALU = mybir.AluOpType
+
+P = 128
+PACK = 4
+K_PASS = P * PACK
+PASSES = K // K_PASS
+HALF = 512
+HALVES = N // HALF
+GROUPS = M // K_PASS
+PAIRS = 2 * GROUPS
+CHUNKS = PAIRS * PASSES
+COLS = 2 * P
+
+
+def tile_gauss_newton_curvature_product_g5_kernel(
+    tc, z, zdot, gain, v, w_words, w_scales, vb, rate, omega, out_0, out_1, out_2
+):
+    nc = tc.nc
+    with ExitStack() as ctx:
+        keep = ctx.enter_context(tc.tile_pool(name="keep", bufs=1))
+        work = ctx.enter_context(tc.tile_pool(name="work", bufs=2))
+        psum = ctx.enter_context(tc.psum_pool(name="psum", bufs=1))
+        ctx.enter_context(tc.manual_schedule())
+
+        z_rows = z.rearrange("(g p t) k -> g p t k", p=P, t=PACK)
+        zdot_rows = zdot.rearrange("(g p t) k -> g p t k", p=P, t=PACK)
+        rate_rows = rate.rearrange("(g p t) n -> g p t n", p=P, t=PACK)
+        out_rows = out_0.rearrange("(g p t) n -> g p t n", p=P, t=PACK)
+        v_rows = v.rearrange("(c p j) n -> c p j n", p=P, j=PACK)
+
+        ident = keep.tile([P, P], F32, name="ident")
+        make_identity(nc, ident[:])
+        w_sc = keep.tile([P, PASSES, N], U8, name="w_sc", align_bytes=64)
+        nc.gpsimd.memset(w_sc[:].rearrange("p c n -> p (c n)").bitcast(I32), 0)
+
+        gain_bf = keep.tile([P, PASSES, PACK], BF16, name="gain_bf")
+        nc.scalar.dma_start(out=gain_bf[:], in_=gain.rearrange("(c p t) -> p c t", p=P, t=PACK))
+        warm = keep.tile([P, 1], F32, name="warm")
+        nc.scalar.activation(out=warm[:], in_=ident[:, 0:1], func=ACT.Tanh)
+
+        z_sb, zdot_sb, v_raw, rate_sb = {}, {}, {}, {}
+
+        def load_rows(store, rows, label, pair, c_lo, c_hi):
+            g, t0 = pair // 2, 2 * (pair % 2)
+            width = (c_hi - c_lo) * K_PASS
+            raw = keep.tile([P, 2, width], BF16, name="%s_%d_%d" % (label, pair, c_lo))
+            nc.sync.dma_start(out=raw[:], in_=rows[g][:, t0 : t0 + 2, c_lo * K_PASS : c_hi * K_PASS])
+            for c in range(c_lo, c_hi):
+                store[PASSES * pair + c] = (raw, c - c_lo)
+
+        def load_v(c, h):
+            raw = keep.tile([P, PACK, HALF], BF16, name="v_raw_%d_%d" % (c, h))
+            nc.sync.dma_start(out=raw[:], in_=v_rows[c][:, :, h * HALF : (h + 1) * HALF])
+            v_raw[c, h] = raw
+
+        def load_rate(pair):
+            g, t0 = pair // 2, 2 * (pair % 2)
+            raw = keep.tile([P, 2, N], BF16, name="rate_%d" % pair)
+            nc.sync.dma_start(out=raw[:], in_=rate_rows[g][:, t0 : t0 + 2, :])
+            rate_sb[pair] = raw
+
+        load_rows(z_sb, z_rows, "z", 0, 0, 1)
+        load_v(0, 0)
+        load_rows(z_sb, z_rows, "z", 0, 1, 2)
+        load_rows(zdot_sb, zdot_rows, "zd", 0, 0, 1)
+        load_v(0, 1)
+        load_rows(z_sb, z_rows, "z", 0, 2, 3)
+        load_rows(zdot_sb, zdot_rows, "zd", 0, 1, 2)
+        load_v(1, 0)
+        w_sb = keep.tile([P, PASSES, 2 * N], U8, name="w_sb", align_bytes=64)
+        nc.sync.dma_start(out=w_sb[:].bitcast(I32), in_=w_words.rearrange("c p b -> p c b").bitcast(I32))
+        for quad in range(4):
+            nc.sync.dma_start(
+                out=w_sc[32 * quad : 32 * quad + 4, :, :].bitcast(I32),
+                in_=w_scales[:, 4 * quad : 4 * quad + 4, :].rearrange("c r n -> r c n").bitcast(I32),
+            )
+        load_v(1, 1)
+        load_rows(zdot_sb, zdot_rows, "zd", 0, 2, 3)
+        load_rows(z_sb, z_rows, "z", 1, 0, PASSES)
+        load_v(2, 0)
+        load_v(2, 1)
+        load_rows(zdot_sb, zdot_rows, "zd", 1, 0, PASSES)
+        vb_sb = keep.tile([P, N], BF16, name="vb_sb")
+        nc.sync.dma_start(out=vb_sb[:], in_=vb.partition_broadcast(P))
+        omega_sb = keep.tile([P, GROUPS, PACK], BF16, name="omega_sb")
+        nc.sync.dma_start(out=omega_sb[:], in_=omega.rearrange("(g p t) -> p g t", p=P, t=PACK))
+        load_rate(0)
+        for pair in range(2, PAIRS):
+            load_rows(z_sb, z_rows, "z", pair, 0, PASSES)
+            load_rows(zdot_sb, zdot_rows, "zd", pair, 0, PASSES)
+            load_rate(pair - 1)
+        load_rate(PAIRS - 1)
+
+        gain_f = keep.tile([P, PASSES, PACK], F32, name="gain_f")
+        neg_gain_f = keep.tile([P, PASSES, PACK], F32, name="neg_gain_f")
+        nc.vector.tensor_copy(out=gain_f[:], in_=gain_bf[:])
+        nc.vector.tensor_scalar(out=neg_gain_f[:], in0=gain_bf[:], scalar1=-1.0, scalar2=None, op0=ALU.mult)
+
+        z_bank, zdot_bank, tanh_z, tanh_sq, slope, rounded, codes, scales = {}, {}, {}, {}, {}, {}, {}, {}
+        v_grouped, v_codes, v_scales, acc, y_sb, y_grouped = {}, {}, {}, {}, {}, {}
+
+        def turn(banks, store, label, s):
+            raw, c_in = store[s]
+            bank = psum.tile([P, 2, COLS], F32, name=label, tag=label, bufs=2)
+            for u in range(2):
+                for a in range(2):
+                    words = raw[:, a, c_in * K_PASS : (c_in + 1) * K_PASS].bitcast(F32)
+                    nc.tensor.transpose(bank[:, u, a * P : (a + 1) * P], words[:, u : 2 * P : 2], ident[:])
+            banks[s] = bank
+
+        def tanh_step(s):
+            th = work.tile([P, PACK, COLS], F32, name="th", tag="th", bufs=3)
+            nc.scalar.activation(
+                out=th[:].rearrange("p (u e) m -> p u e m", e=2),
+                in_=z_bank[s][:].bitcast(BF16).rearrange("p u (m e) -> p u e m", e=2),
+                func=ACT.Tanh,
+            )
+            tanh_z[s] = th
+
+        def square_step(s):
+            sq = work.tile([P, PACK, COLS], F32, name="sq", tag="sq", bufs=2)
+            nc.scalar.activation(out=sq[:], in_=tanh_z[s][:], func=ACT.Square)
+            tanh_sq[s] = sq
+
+        def slope_step(s):
+            c = s % PASSES
+            sl = work.tile([P, PACK, COLS], F32, name="sl", tag="sl", bufs=3)
+            for t in range(PACK):
+                nc.scalar.activation(
+                    out=sl[:, t, :], in_=tanh_sq[s][:, t, :], func=ACT.Identity,
+                    scale=neg_gain_f[:, c, t : t + 1], bias=gain_f[:, c, t : t + 1],
+                )
+            slope[s] = sl
+
+        def h_step(s):
+            c = s % PASSES
+            hb = work.tile([P, 2, COLS, PACK], BF16, name="hb", tag="hb", bufs=2, align_bytes=64)
+            nc.vector.tensor_tensor(
+                out=hb[:, 0, :, :].rearrange("p (q i) t -> p q t i", i=4),
+                in0=tanh_z[s][:].rearrange("p t (q i) -> p q t i", i=4),
+                in1=gain_f[:, c, :].rearrange("p (q t i) -> p q t i", q=1, i=1).to_broadcast([P, COLS // 4, PACK, 4]),
+                op=ALU.mult,
+            )
+            rounded[s] = hb
+
+        def hdot_step(s):
+            nc.vector.tensor_tensor(
+                out=rounded[s][:, 1, :, :].rearrange("p m (u e) -> p m u e", e=2),
+                in0=zdot_bank[s][:].bitcast(BF16).rearrange("p u (m e) -> p m u e", e=2),
+                in1=slope[s][:].rearrange("p (u e) m -> p m u e", e=2),
+                op=ALU.mult,
+            )
+
+        def quantise_step(s):
+            hc = work.tile([P, 2 * COLS], U32, name="hc", tag="hc", bufs=3, align_bytes=64)
+            hs = work.tile([P, 2 * COLS], U8, name="hs", tag="hs", bufs=3, align_bytes=64)
+            nc.vector.quantize_mx(
+                out=hc[:].bitcast(FP8X4), scales=hs[:], in_=rounded[s][:].rearrange("p k m t -> p (k m t)")
+            )
+            codes[s], scales[s] = hc, hs
+
+        def interleave(on_vector, out, in_):
+            out = out.rearrange("p (q i) t -> p q t i", i=4)
+            in_ = in_.rearrange("p t (q i) -> p q t i", i=4)
+            if on_vector:
+                nc.vector.tensor_copy(out=out, in_=in_)
+            else:
+                nc.scalar.copy(out=out, in_=in_)
+
+        def v_interleave(c, h, on_vector):
+            vg = work.tile([P, HALF, PACK], BF16, name="vg", tag="vg", bufs=3, align_bytes=64)
+            interleave(on_vector, vg[:], v_raw[c, h][:])
+            v_grouped[c, h] = vg
+
+        def v_quantise(c, h):
+            vc = keep.tile([P, HALF], U32, name="vc_%d_%d" % (c, h), align_bytes=64)
+            vs = keep.tile([P, HALF], U8, name="vs_%d_%d" % (c, h), align_bytes=64)
+            nc.vector.quantize_mx(
+                out=vc[:].bitcast(FP8X4), scales=vs[:], in_=v_grouped[c, h][:].rearrange("p n t -> p (n t)")
+            )
+            v_codes[c, h], v_scales[c, h] = vc, vs
+
+        def multiply(s, h):
+            pair, c = divmod(s, PASSES)
+            for a in range(2):
+                if c == 0:
+                    acc[pair, a, h] = psum.tile([P, HALF], F32, name="acc", tag="acc_%d_%d" % (a, h), bufs=1)
+                h_cols = slice(a * P, (a + 1) * P)
+                hdot_cols = slice(COLS + a * P, COLS + (a + 1) * P)
+                nc.tensor.matmul_mx(
+                    out=acc[pair, a, h][:],
+                    lhsT=codes[s][:, hdot_cols].bitcast(FP8X4), lhsT_scale=scales[s][:, hdot_cols],
+                    rhs=w_sb[:, c, 2 * h * HALF : 2 * (h + 1) * HALF].bitcast(FP4X4),
+                    rhs_scale=w_sc[:, c, h * HALF : (h + 1) * HALF],
+                    start=(c == 0), stop=False,
+                )
+                nc.tensor.matmul_mx(
+                    out=acc[pair, a, h][:],
+                    lhsT=codes[s][:, h_cols].bitcast(FP8X4), lhsT_scale=scales[s][:, h_cols],
+                    rhs=v_codes[c, h][:].bitcast(FP8X4), rhs_scale=v_scales[c, h][:],
+                    start=False, stop=(c == PASSES - 1),
+                )
+
+        for g in range(GROUPS):
+            for h in range(HALVES):
+                y_sb[g, h] = keep.tile([P, PACK, HALF], F32, name="y_%d_%d" % (g, h))
+        y_codes = [keep.tile([P, N], U32, name="y_codes_%d" % g, align_bytes=64) for g in range(GROUPS)]
+        y_scales = [keep.tile([P, N], U8, name="y_scales_%d" % g, align_bytes=64) for g in range(GROUPS)]
+
+        def add_bias(pair, a, h):
+            g, t = pair // 2, 2 * (pair % 2) + a
+            nc.vector.tensor_tensor(
+                out=y_sb[g, h][:, t, :], in0=acc[pair, a, h][:], in1=vb_sb[:, h * HALF : (h + 1) * HALF], op=ALU.add
+            )
+
+        def weigh(pair, a, h):
+            g, t = pair // 2, 2 * (pair % 2) + a
+            nc.vector.scalar_tensor_tensor(
+                out=y_sb[g, h][:, t, :], in0=y_sb[g, h][:, t, :], scalar=omega_sb[:, g, t : t + 1],
+                in1=rate_sb[pair][:, a, h * HALF : (h + 1) * HALF], op0=ALU.mult, op1=ALU.mult,
+            )
+
+        def store_y(pair, h):
+            g, t0 = pair // 2, 2 * (pair % 2)
+            nc.sync.dma_start(
+                out=out_rows[g][:, t0 : t0 + 2, h * HALF : (h + 1) * HALF], in_=y_sb[g, h][:, t0 : t0 + 2, :]
+            )
+
+        def y_interleave(g, lo, hi, on_vector):
+            h = lo // HALF
+            yg = work.tile([P, hi - lo, PACK], BF16, name="yg", tag="yg", bufs=3, align_bytes=64)
+            interleave(on_vector, yg[:], y_sb[g, h][:, :, lo - h * HALF : hi - h * HALF])
+            y_grouped[g, lo] = yg
+
+        def y_quantise(g, lo, hi):
+            nc.vector.quantize_mx(
+                out=y_codes[g][:, lo:hi].bitcast(FP8X4), scales=y_scales[g][:, lo:hi],
+                in_=y_grouped[g, lo][:].rearrange("p n t -> p (n t)"),
+            )
+
+        def store_codes(g, lo, hi):
+            nc.sync.dma_start(
+                out=out_1[g].rearrange("p n t -> p (n t)").bitcast(I32)[:, lo:hi], in_=y_codes[g][:, lo:hi].bitcast(I32)
+            )
+
+        def store_scales(g, queues):
+            for quad in range(4):
+                queues[quad].dma_start(
+                    out=out_2[g, 4 * quad : 4 * quad + 4, :].bitcast(I32),
+                    in_=y_scales[g][32 * quad : 32 * quad + 4, :].bitcast(I32),
+                )
+
+        turn(z_bank, z_sb, "zb", 0)
+        turn(z_bank, z_sb, "zb", 1)
+        turn(zdot_bank, zdot_sb, "zdb", 0)
+        tanh_step(0)
+        v_interleave(0, 0, True)
+        h_step(0)
+        v_interleave(0, 1, True)
+        v_quantise(0, 0)
+
+        for s in range(CHUNKS):
+            done, phase = divmod(s - PASSES, PASSES)
+            busy = done >= 0
+            if busy and phase == 1:
+                add_bias(done, 1, 1)
+            if s + 2 < CHUNKS:
+                turn(z_bank, z_sb, "zb", s + 2)
+            if s >= 1:
+                multiply(s - 1, 0)
+            if s + 1 < CHUNKS:
+                turn(zdot_bank, zdot_sb, "zdb", s + 1)
+            if s >= 1:
+                multiply(s - 1, 1)
+
+            square_step(s)
+            if s + 1 < CHUNKS:
+                tanh_step(s + 1)
+            slope_step(s)
+            if s + 1 < PASSES:
+                v_interleave(s + 1, 1, False)
+            if s == 9 or s == 10:
+                y_interleave(0, (s - 9) * HALF, (s - 8) * HALF, False)
+
+            if s < PASSES:
+                v_quantise(s, 1)
+            if s + 1 < PASSES:
+                v_interleave(s + 1, 0, True)
+            hdot_step(s)
+            if s + 1 < CHUNKS:
+                h_step(s + 1)
+            if busy and phase == 0:
+                add_bias(done, 0, 0)
+            if busy and phase >= 1:
+                weigh(done, 0, phase - 1)
+            quantise_step(s)
+            if s + 1 < PASSES:
+                v_quantise(s + 1, 0)
+            if busy and phase == 0:
+                add_bias(done, 1, 0)
+                add_bias(done, 0, 1)
+            if busy and phase >= 1:
+                weigh(done, 1, phase - 1)
+                store_y(done, phase - 1)
+            if s == 10 or s == 11:
+                y_quantise(0, (s - 10) * HALF, (s - 9) * HALF)
+                store_codes(0, (s - 10) * HALF, (s - 9) * HALF)
+            if s == 11:
+                store_scales(0, [nc.sync] * 4)
+
+        last = PAIRS - 1
+        multiply(CHUNKS - 1, 0)
+        multiply(CHUNKS - 1, 1)
+        for h in range(HALVES):
+            add_bias(last, 0, h)
+            add_bias(last, 1, h)
+            weigh(last, 0, h)
+            weigh(last, 1, h)
+            store_y(last, h)
+            if h == 0:
+                y_interleave(1, 0, HALF, False)
+        y_interleave(1, 768, N, False)
+        y_quantise(1, 0, HALF)
+        store_codes(1, 0, HALF)
+        y_interleave(1, HALF, 768, True)
+        y_quantise(1, HALF, 768)
+        y_quantise(1, 768, N)
+        store_codes(1, HALF, N)
+        store_scales(1, [nc.scalar, nc.sync, nc.scalar, nc.sync])

@@ -80,9 +80,10 @@ def tile_gauss_newton_curvature_product_g5_kernel(
         load_rows(z_sb, z_rows, "z", 0, 1, 2)
         load_rows(zdot_sb, zdot_rows, "zd", 0, 0, 1)
         load_v(0, 1)
+        load_v(1, 1)
+        load_v(1, 0)
         load_rows(z_sb, z_rows, "z", 0, 2, 3)
         load_rows(zdot_sb, zdot_rows, "zd", 0, 1, 2)
-        load_v(1, 0)
         w_sb = keep.tile([P, PASSES, 2 * N], U8, name="w_sb", align_bytes=64)
         nc.sync.dma_start(out=w_sb[:].bitcast(I32), in_=w_words.rearrange("c p b -> p c b").bitcast(I32))
         for quad in range(4):
@@ -90,11 +91,10 @@ def tile_gauss_newton_curvature_product_g5_kernel(
                 out=w_sc[32 * quad : 32 * quad + 4, :, :].bitcast(I32),
                 in_=w_scales[:, 4 * quad : 4 * quad + 4, :].rearrange("c r n -> r c n").bitcast(I32),
             )
-        load_v(1, 1)
+        load_v(2, 1)
+        load_v(2, 0)
         load_rows(zdot_sb, zdot_rows, "zd", 0, 2, 3)
         load_rows(z_sb, z_rows, "z", 1, 0, PASSES)
-        load_v(2, 0)
-        load_v(2, 1)
         load_rows(zdot_sb, zdot_rows, "zd", 1, 0, PASSES)
         vb_sb = keep.tile([P, N], BF16, name="vb_sb")
         nc.sync.dma_start(out=vb_sb[:], in_=vb.partition_broadcast(P))
@@ -112,6 +112,9 @@ def tile_gauss_newton_curvature_product_g5_kernel(
         nc.vector.tensor_copy(out=gain_f[:], in_=gain_bf[:])
         nc.vector.tensor_scalar(out=neg_gain_f[:], in0=gain_bf[:], scalar1=-1.0, scalar2=None, op0=ALU.mult)
 
+        gain_row = keep.tile([P, PASSES, COLS, PACK], BF16, name="gain_row")
+        nc.vector.tensor_copy(out=gain_row[:], in_=gain_bf[:].rearrange("p c (m t) -> p c m t", m=1).to_broadcast([P, PASSES, COLS, PACK]))
+
         z_bank, zdot_bank, tanh_z, tanh_sq, slope, rounded, codes, scales = {}, {}, {}, {}, {}, {}, {}, {}
         v_grouped, v_codes, v_scales, acc, y_sb, y_grouped = {}, {}, {}, {}, {}, {}
 
@@ -125,22 +128,22 @@ def tile_gauss_newton_curvature_product_g5_kernel(
             banks[s] = bank
 
         def tanh_step(s):
-            th = work.tile([P, PACK, COLS], F32, name="th", tag="th", bufs=3)
-            nc.scalar.activation(
-                out=th[:].rearrange("p (u e) m -> p u e m", e=2),
-                in_=z_bank[s][:].bitcast(BF16).rearrange("p u (m e) -> p u e m", e=2),
-                func=ACT.Tanh,
-            )
+            th = work.tile([P, 2, 2 * COLS], F32, name="th", tag="th", bufs=3)
+            nc.scalar.activation(out=th[:], in_=z_bank[s][:].bitcast(BF16), func=ACT.Tanh)
             tanh_z[s] = th
 
         def square_step(s):
             sq = work.tile([P, PACK, COLS], F32, name="sq", tag="sq", bufs=2)
-            nc.scalar.activation(out=sq[:], in_=tanh_z[s][:], func=ACT.Square)
+            nc.scalar.activation(
+                out=sq[:].rearrange("p (u e) m -> p u e m", e=2),
+                in_=tanh_z[s][:].rearrange("p u (m e) -> p u e m", e=2),
+                func=ACT.Square,
+            )
             tanh_sq[s] = sq
 
         def slope_step(s):
             c = s % PASSES
-            sl = work.tile([P, PACK, COLS], F32, name="sl", tag="sl", bufs=3)
+            sl = work.tile([P, PACK, COLS], F32, name="sl", tag="sl", bufs=2)
             for t in range(PACK):
                 nc.scalar.activation(
                     out=sl[:, t, :], in_=tanh_sq[s][:, t, :], func=ACT.Identity,
@@ -151,10 +154,11 @@ def tile_gauss_newton_curvature_product_g5_kernel(
         def h_step(s):
             c = s % PASSES
             hb = work.tile([P, 2, COLS, PACK], BF16, name="hb", tag="hb", bufs=2, align_bytes=64)
-            nc.vector.tensor_tensor(
-                out=hb[:, 0, :, :].rearrange("p (q i) t -> p q t i", i=4),
-                in0=tanh_z[s][:].rearrange("p t (q i) -> p q t i", i=4),
-                in1=gain_f[:, c, :].rearrange("p (q t i) -> p q t i", q=1, i=1).to_broadcast([P, COLS // 4, PACK, 4]),
+            engine = nc.gpsimd if s > PASSES else nc.vector
+            engine.tensor_tensor(
+                out=hb[:, 0, :, :].rearrange("p m (u e) -> p m u e", e=2),
+                in0=tanh_z[s][:].rearrange("p u (m e) -> p m u e", e=2),
+                in1=gain_row[:, c, :, :].rearrange("p m (u e) -> p m u e", e=2),
                 op=ALU.mult,
             )
             rounded[s] = hb
@@ -279,6 +283,7 @@ def tile_gauss_newton_curvature_product_g5_kernel(
             done, phase = divmod(s - PASSES, PASSES)
             busy = done >= 0
             if busy and phase == 1:
+                add_bias(done, 0, 1)
                 add_bias(done, 1, 1)
             if s + 2 < CHUNKS:
                 turn(z_bank, z_sb, "zb", s + 2)
@@ -295,8 +300,8 @@ def tile_gauss_newton_curvature_product_g5_kernel(
             slope_step(s)
             if s + 1 < PASSES:
                 v_interleave(s + 1, 1, False)
-            if s == 9 or s == 10:
-                y_interleave(0, (s - 9) * HALF, (s - 8) * HALF, False)
+            if s == 8 or s == 10:
+                y_interleave(0, (s - 8) // 2 * HALF, (s - 6) // 2 * HALF, False)
 
             if s < PASSES:
                 v_quantise(s, 1)
@@ -307,23 +312,24 @@ def tile_gauss_newton_curvature_product_g5_kernel(
                 h_step(s + 1)
             if busy and phase == 0:
                 add_bias(done, 0, 0)
+                add_bias(done, 1, 0)
+            if s == 9:
+                y_quantise(0, 0, HALF)
+                store_codes(0, 0, HALF)
             if busy and phase >= 1:
                 weigh(done, 0, phase - 1)
+                if s + 1 < CHUNKS:
+                    weigh(done, 1, phase - 1)
+                    store_y(done, phase - 1)
             quantise_step(s)
             if s + 1 < PASSES:
                 v_quantise(s + 1, 0)
-            if busy and phase == 0:
-                add_bias(done, 1, 0)
-                add_bias(done, 0, 1)
-            if busy and phase >= 1:
-                weigh(done, 1, phase - 1)
-                store_y(done, phase - 1)
-            if s == 10 or s == 11:
-                y_quantise(0, (s - 10) * HALF, (s - 9) * HALF)
-                store_codes(0, (s - 10) * HALF, (s - 9) * HALF)
-            if s == 11:
-                store_scales(0, [nc.sync] * 4)
 
+        weigh(PAIRS - 2, 1, 1)
+        store_y(PAIRS - 2, 1)
+        y_quantise(0, HALF, N)
+        store_codes(0, HALF, N)
+        store_scales(0, [nc.sync] * 4)
         last = PAIRS - 1
         multiply(CHUNKS - 1, 0)
         multiply(CHUNKS - 1, 1)

@@ -26,6 +26,9 @@ GROUPS = M // K_PASS
 PAIRS = 2 * GROUPS
 CHUNKS = PAIRS * PASSES
 COLS = 2 * P
+QUADRANTS = 4
+RUN = 4
+QUARTER = HALF // 2
 
 
 def tile_gauss_newton_curvature_product_g5_kernel(
@@ -42,7 +45,10 @@ def tile_gauss_newton_curvature_product_g5_kernel(
         zdot_rows = zdot.rearrange("(g p t) k -> g p t k", p=P, t=PACK)
         rate_rows = rate.rearrange("(g p t) n -> g p t n", p=P, t=PACK)
         out_rows = out_0.rearrange("(g p t) n -> g p t n", p=P, t=PACK)
-        v_rows = v.rearrange("(c p j) n -> c p j n", p=P, j=PACK)
+        v_rows = v.rearrange("(c p t) n -> c p t n", p=P, t=PACK)
+
+        def tiles_of(pair):
+            return pair // 2, 2 * (pair % 2)
 
         ident = keep.tile([P, P], F32, name="ident")
         make_identity(nc, ident[:])
@@ -51,301 +57,325 @@ def tile_gauss_newton_curvature_product_g5_kernel(
 
         gain_bf = keep.tile([P, PASSES, PACK], BF16, name="gain_bf")
         nc.scalar.dma_start(out=gain_bf[:], in_=gain.rearrange("(c p t) -> p c t", p=P, t=PACK))
-        warm = keep.tile([P, 1], F32, name="warm")
-        nc.scalar.activation(out=warm[:], in_=ident[:, 0:1], func=ACT.Tanh)
 
-        z_sb, zdot_sb, v_raw, rate_sb = {}, {}, {}, {}
+        z_sb, zdot_sb, v_raw, w_sb, rate_sb = {}, {}, {}, {}, {}
 
-        def load_rows(store, rows, label, pair, c_lo, c_hi):
-            g, t0 = pair // 2, 2 * (pair % 2)
-            width = (c_hi - c_lo) * K_PASS
-            raw = keep.tile([P, 2, width], BF16, name="%s_%d_%d" % (label, pair, c_lo))
+        def load_rows(chunks, rows, label, pair, c_lo, c_hi):
+            g, t0 = tiles_of(pair)
+            raw = keep.tile([P, 2, (c_hi - c_lo) * K_PASS], BF16, name="%s_%d_%d" % (label, pair, c_lo))
             nc.sync.dma_start(out=raw[:], in_=rows[g][:, t0 : t0 + 2, c_lo * K_PASS : c_hi * K_PASS])
             for c in range(c_lo, c_hi):
-                store[PASSES * pair + c] = (raw, c - c_lo)
+                chunks[PASSES * pair + c] = raw[:, :, (c - c_lo) * K_PASS : (c - c_lo + 1) * K_PASS]
 
-        def load_v(c, h):
-            raw = keep.tile([P, PACK, HALF], BF16, name="v_raw_%d_%d" % (c, h))
-            nc.sync.dma_start(out=raw[:], in_=v_rows[c][:, :, h * HALF : (h + 1) * HALF])
-            v_raw[c, h] = raw
+        def load_z(pair, c_lo=0, c_hi=PASSES):
+            load_rows(z_sb, z_rows, "z", pair, c_lo, c_hi)
+
+        def load_zdot(pair, c_lo=0, c_hi=PASSES):
+            load_rows(zdot_sb, zdot_rows, "zd", pair, c_lo, c_hi)
+
+        def load_v(c, h_lo=0, h_hi=HALVES):
+            raw = keep.tile([P, PACK, (h_hi - h_lo) * HALF], BF16, name="v_raw_%d_%d" % (c, h_lo))
+            nc.sync.dma_start(out=raw[:], in_=v_rows[c][:, :, h_lo * HALF : h_hi * HALF])
+            for h in range(h_lo, h_hi):
+                v_raw[c, h] = raw[:, :, (h - h_lo) * HALF : (h - h_lo + 1) * HALF]
+
+        def load_w(c_lo, c_hi):
+            raw = keep.tile([P, c_hi - c_lo, 2 * N], U8, name="w_%d" % c_lo, align_bytes=64)
+            nc.sync.dma_start(out=raw[:].bitcast(I32), in_=w_words[c_lo:c_hi].rearrange("c p b -> p c b").bitcast(I32))
+            for c in range(c_lo, c_hi):
+                w_sb[c] = raw[:, c - c_lo, :]
 
         def load_rate(pair):
-            g, t0 = pair // 2, 2 * (pair % 2)
+            g, t0 = tiles_of(pair)
             raw = keep.tile([P, 2, N], BF16, name="rate_%d" % pair)
             nc.sync.dma_start(out=raw[:], in_=rate_rows[g][:, t0 : t0 + 2, :])
             rate_sb[pair] = raw
 
-        load_rows(z_sb, z_rows, "z", 0, 0, 1)
-        load_v(0, 0)
-        load_rows(z_sb, z_rows, "z", 0, 1, 2)
-        load_rows(zdot_sb, zdot_rows, "zd", 0, 0, 1)
-        load_v(0, 1)
-        load_v(1, 1)
-        load_v(1, 0)
-        load_rows(z_sb, z_rows, "z", 0, 2, 3)
-        load_rows(zdot_sb, zdot_rows, "zd", 0, 1, 2)
-        w_sb = keep.tile([P, PASSES, 2 * N], U8, name="w_sb", align_bytes=64)
-        nc.sync.dma_start(out=w_sb[:].bitcast(I32), in_=w_words.rearrange("c p b -> p c b").bitcast(I32))
-        for quad in range(4):
+        load_z(0, 0, 1)
+        load_v(0, 0, 1)
+        load_z(0, 1, PASSES)
+        load_zdot(0, 0, 1)
+        load_v(0, 1, HALVES)
+        load_v(1)
+        load_zdot(0, 1, PASSES)
+        load_w(0, 1)
+        for quad in range(QUADRANTS):
             nc.sync.dma_start(
                 out=w_sc[32 * quad : 32 * quad + 4, :, :].bitcast(I32),
                 in_=w_scales[:, 4 * quad : 4 * quad + 4, :].rearrange("c r n -> r c n").bitcast(I32),
             )
-        load_v(2, 1)
-        load_v(2, 0)
-        load_rows(zdot_sb, zdot_rows, "zd", 0, 2, 3)
-        load_rows(z_sb, z_rows, "z", 1, 0, PASSES)
-        load_rows(zdot_sb, zdot_rows, "zd", 1, 0, PASSES)
+        load_z(1, 0, 1)
+        load_v(2)
+        load_w(1, PASSES)
+        load_z(1, 1, PASSES)
+        load_zdot(1)
         vb_sb = keep.tile([P, N], BF16, name="vb_sb")
         nc.sync.dma_start(out=vb_sb[:], in_=vb.partition_broadcast(P))
+        load_z(2)
         omega_sb = keep.tile([P, GROUPS, PACK], BF16, name="omega_sb")
         nc.sync.dma_start(out=omega_sb[:], in_=omega.rearrange("(g p t) -> p g t", p=P, t=PACK))
         load_rate(0)
-        for pair in range(2, PAIRS):
-            load_rows(z_sb, z_rows, "z", pair, 0, PASSES)
-            load_rows(zdot_sb, zdot_rows, "zd", pair, 0, PASSES)
-            load_rate(pair - 1)
-        load_rate(PAIRS - 1)
+        load_zdot(2)
+        load_z(3)
+        load_rate(1)
+        load_zdot(3)
+        load_rate(2)
+        load_rate(3)
 
         gain_f = keep.tile([P, PASSES, PACK], F32, name="gain_f")
         neg_gain_f = keep.tile([P, PASSES, PACK], F32, name="neg_gain_f")
         nc.vector.tensor_copy(out=gain_f[:], in_=gain_bf[:])
         nc.vector.tensor_scalar(out=neg_gain_f[:], in0=gain_bf[:], scalar1=-1.0, scalar2=None, op0=ALU.mult)
-
         gain_row = keep.tile([P, PASSES, COLS, PACK], BF16, name="gain_row")
-        nc.vector.tensor_copy(out=gain_row[:], in_=gain_bf[:].rearrange("p c (m t) -> p c m t", m=1).to_broadcast([P, PASSES, COLS, PACK]))
+        nc.vector.tensor_copy(
+            out=gain_row[:], in_=gain_bf[:].rearrange("p c (m t) -> p c m t", m=1).to_broadcast([P, PASSES, COLS, PACK])
+        )
 
-        z_bank, zdot_bank, tanh_z, tanh_sq, slope, rounded, codes, scales = {}, {}, {}, {}, {}, {}, {}, {}
-        v_grouped, v_codes, v_scales, acc, y_sb, y_grouped = {}, {}, {}, {}, {}, {}
+        z_bank, zdot_bank, tanh_z, tanh_sq, slope, h_bf, hdot_bf, codes, scales = {}, {}, {}, {}, {}, {}, {}, {}, {}
 
-        def turn(banks, store, label, s):
-            raw, c_in = store[s]
+        def turn(banks, chunks, label, s):
             bank = psum.tile([P, 2, COLS], F32, name=label, tag=label, bufs=2)
             for u in range(2):
                 for a in range(2):
-                    words = raw[:, a, c_in * K_PASS : (c_in + 1) * K_PASS].bitcast(F32)
+                    words = chunks[s][:, a, :].bitcast(F32)
                     nc.tensor.transpose(bank[:, u, a * P : (a + 1) * P], words[:, u : 2 * P : 2], ident[:])
             banks[s] = bank
 
+        def turn_z(s):
+            turn(z_bank, z_sb, "zb", s)
+
+        def turn_zdot(s):
+            turn(zdot_bank, zdot_sb, "zdb", s)
+
         def tanh_step(s):
-            th = work.tile([P, 2, 2 * COLS], F32, name="th", tag="th", bufs=3)
-            nc.scalar.activation(out=th[:], in_=z_bank[s][:].bitcast(BF16), func=ACT.Tanh)
-            tanh_z[s] = th
+            tanh_z[s] = work.tile([P, 2, 2 * COLS], F32, name="th", tag="th", bufs=3)
+            nc.scalar.activation(out=tanh_z[s][:], in_=z_bank[s][:].bitcast(BF16), func=ACT.Tanh)
 
         def square_step(s):
-            sq = work.tile([P, PACK, COLS], F32, name="sq", tag="sq", bufs=2)
+            tanh_sq[s] = work.tile([P, PACK, COLS], F32, name="sq", tag="sq", bufs=2)
             nc.scalar.activation(
-                out=sq[:].rearrange("p (u e) m -> p u e m", e=2),
+                out=tanh_sq[s][:].rearrange("p (u e) m -> p u e m", e=2),
                 in_=tanh_z[s][:].rearrange("p u (m e) -> p u e m", e=2),
                 func=ACT.Square,
             )
-            tanh_sq[s] = sq
 
         def slope_step(s):
             c = s % PASSES
-            sl = work.tile([P, PACK, COLS], F32, name="sl", tag="sl", bufs=2)
+            slope[s] = work.tile([P, PACK, COLS], F32, name="sl", tag="sl", bufs=3)
             for t in range(PACK):
                 nc.scalar.activation(
-                    out=sl[:, t, :], in_=tanh_sq[s][:, t, :], func=ACT.Identity,
+                    out=slope[s][:, t, :], in_=tanh_sq[s][:, t, :], func=ACT.Identity,
                     scale=neg_gain_f[:, c, t : t + 1], bias=gain_f[:, c, t : t + 1],
                 )
-            slope[s] = sl
 
-        def h_step(s):
-            c = s % PASSES
-            hb = work.tile([P, 2, COLS, PACK], BF16, name="hb", tag="hb", bufs=2, align_bytes=64)
-            engine = nc.gpsimd if s > PASSES else nc.vector
+        def h_step(s, lo, hi, engine):
+            if lo == 0:
+                h_bf[s] = work.tile([P, COLS, PACK], BF16, name="hb", tag="hb", bufs=2, align_bytes=64)
             engine.tensor_tensor(
-                out=hb[:, 0, :, :].rearrange("p m (u e) -> p m u e", e=2),
-                in0=tanh_z[s][:].rearrange("p u (m e) -> p m u e", e=2),
-                in1=gain_row[:, c, :, :].rearrange("p m (u e) -> p m u e", e=2),
+                out=h_bf[s][:, lo:hi, :].rearrange("p m (u e) -> p m u e", e=2),
+                in0=tanh_z[s][:, :, 2 * lo : 2 * hi].rearrange("p u (m e) -> p m u e", e=2),
+                in1=gain_row[:, s % PASSES, lo:hi, :].rearrange("p m (u e) -> p m u e", e=2),
                 op=ALU.mult,
             )
-            rounded[s] = hb
 
         def hdot_step(s):
+            hdot_bf[s] = work.tile([P, COLS, PACK], BF16, name="hb", tag="hd", bufs=2, align_bytes=64)
             nc.vector.tensor_tensor(
-                out=rounded[s][:, 1, :, :].rearrange("p m (u e) -> p m u e", e=2),
+                out=hdot_bf[s][:].rearrange("p m (u e) -> p m u e", e=2),
                 in0=zdot_bank[s][:].bitcast(BF16).rearrange("p u (m e) -> p m u e", e=2),
                 in1=slope[s][:].rearrange("p (u e) m -> p m u e", e=2),
                 op=ALU.mult,
             )
 
+        def quantise(words, scale_bytes, values):
+            nc.vector.quantize_mx(out=words.bitcast(FP8X4), scales=scale_bytes, in_=values.rearrange("p n t -> p (n t)"))
+
         def quantise_step(s):
-            hc = work.tile([P, 2 * COLS], U32, name="hc", tag="hc", bufs=3, align_bytes=64)
-            hs = work.tile([P, 2 * COLS], U8, name="hs", tag="hs", bufs=3, align_bytes=64)
-            nc.vector.quantize_mx(
-                out=hc[:].bitcast(FP8X4), scales=hs[:], in_=rounded[s][:].rearrange("p k m t -> p (k m t)")
-            )
-            codes[s], scales[s] = hc, hs
+            codes[s] = work.tile([P, 2, COLS], U32, name="hc", tag="hc", bufs=3, align_bytes=64)
+            scales[s] = work.tile([P, 2, COLS], U8, name="hs", tag="hs", bufs=3, align_bytes=64)
+            quantise(codes[s][:, 0, :], scales[s][:, 0, :], h_bf[s][:])
+            quantise(codes[s][:, 1, :], scales[s][:, 1, :], hdot_bf[s][:])
 
-        def interleave(on_vector, out, in_):
-            out = out.rearrange("p (q i) t -> p q t i", i=4)
-            in_ = in_.rearrange("p t (q i) -> p q t i", i=4)
-            if on_vector:
-                nc.vector.tensor_copy(out=out, in_=in_)
-            else:
-                nc.scalar.copy(out=out, in_=in_)
+        def interleave(copy, out, in_):
+            copy(out=out.rearrange("p (q i) t -> p q t i", i=RUN), in_=in_.rearrange("p t (q i) -> p q t i", i=RUN))
 
-        def v_interleave(c, h, on_vector):
-            vg = work.tile([P, HALF, PACK], BF16, name="vg", tag="vg", bufs=3, align_bytes=64)
-            interleave(on_vector, vg[:], v_raw[c, h][:])
-            v_grouped[c, h] = vg
+        v_bf, v_codes, v_scales, acc = {}, {}, {}, {}
+
+        def v_interleave(c, h, copy, lo=0, hi=HALF):
+            if lo == 0:
+                v_bf[c, h] = work.tile([P, HALF, PACK], BF16, name="vg", tag="vg", bufs=3, align_bytes=64)
+            interleave(copy, v_bf[c, h][:, lo:hi, :], v_raw[c, h][:, :, lo:hi])
 
         def v_quantise(c, h):
-            vc = keep.tile([P, HALF], U32, name="vc_%d_%d" % (c, h), align_bytes=64)
-            vs = keep.tile([P, HALF], U8, name="vs_%d_%d" % (c, h), align_bytes=64)
-            nc.vector.quantize_mx(
-                out=vc[:].bitcast(FP8X4), scales=vs[:], in_=v_grouped[c, h][:].rearrange("p n t -> p (n t)")
-            )
-            v_codes[c, h], v_scales[c, h] = vc, vs
+            v_codes[c, h] = keep.tile([P, HALF], U32, name="vc_%d_%d" % (c, h), align_bytes=64)
+            v_scales[c, h] = keep.tile([P, HALF], U8, name="vs_%d_%d" % (c, h), align_bytes=64)
+            quantise(v_codes[c, h][:], v_scales[c, h][:], v_bf[c, h][:])
 
         def multiply(s, h):
             pair, c = divmod(s, PASSES)
             for a in range(2):
                 if c == 0:
                     acc[pair, a, h] = psum.tile([P, HALF], F32, name="acc", tag="acc_%d_%d" % (a, h), bufs=1)
-                h_cols = slice(a * P, (a + 1) * P)
-                hdot_cols = slice(COLS + a * P, COLS + (a + 1) * P)
+                tile_cols = slice(a * P, (a + 1) * P)
                 nc.tensor.matmul_mx(
                     out=acc[pair, a, h][:],
-                    lhsT=codes[s][:, hdot_cols].bitcast(FP8X4), lhsT_scale=scales[s][:, hdot_cols],
-                    rhs=w_sb[:, c, 2 * h * HALF : 2 * (h + 1) * HALF].bitcast(FP4X4),
-                    rhs_scale=w_sc[:, c, h * HALF : (h + 1) * HALF],
+                    lhsT=codes[s][:, 0, tile_cols].bitcast(FP8X4), lhsT_scale=scales[s][:, 0, tile_cols],
+                    rhs=v_codes[c, h][:].bitcast(FP8X4), rhs_scale=v_scales[c, h][:],
                     start=(c == 0), stop=False,
                 )
                 nc.tensor.matmul_mx(
                     out=acc[pair, a, h][:],
-                    lhsT=codes[s][:, h_cols].bitcast(FP8X4), lhsT_scale=scales[s][:, h_cols],
-                    rhs=v_codes[c, h][:].bitcast(FP8X4), rhs_scale=v_scales[c, h][:],
+                    lhsT=codes[s][:, 1, tile_cols].bitcast(FP8X4), lhsT_scale=scales[s][:, 1, tile_cols],
+                    rhs=w_sb[c][:, 2 * h * HALF : 2 * (h + 1) * HALF].bitcast(FP4X4),
+                    rhs_scale=w_sc[:, c, h * HALF : (h + 1) * HALF],
                     start=False, stop=(c == PASSES - 1),
                 )
 
+        y_sb, y_bf, y_codes, y_scales = {}, {}, {}, {}
         for g in range(GROUPS):
             for h in range(HALVES):
                 y_sb[g, h] = keep.tile([P, PACK, HALF], F32, name="y_%d_%d" % (g, h))
-        y_codes = [keep.tile([P, N], U32, name="y_codes_%d" % g, align_bytes=64) for g in range(GROUPS)]
-        y_scales = [keep.tile([P, N], U8, name="y_scales_%d" % g, align_bytes=64) for g in range(GROUPS)]
+            y_codes[g] = keep.tile([P, N], U32, name="y_codes_%d" % g, align_bytes=64)
+            y_scales[g] = keep.tile([P, N], U8, name="y_scales_%d" % g, align_bytes=64)
 
         def add_bias(pair, a, h):
-            g, t = pair // 2, 2 * (pair % 2) + a
+            g, t0 = tiles_of(pair)
             nc.vector.tensor_tensor(
-                out=y_sb[g, h][:, t, :], in0=acc[pair, a, h][:], in1=vb_sb[:, h * HALF : (h + 1) * HALF], op=ALU.add
+                out=y_sb[g, h][:, t0 + a, :], in0=acc[pair, a, h][:], in1=vb_sb[:, h * HALF : (h + 1) * HALF], op=ALU.add
             )
 
         def weigh(pair, a, h):
-            g, t = pair // 2, 2 * (pair % 2) + a
+            g, t0 = tiles_of(pair)
             nc.vector.scalar_tensor_tensor(
-                out=y_sb[g, h][:, t, :], in0=y_sb[g, h][:, t, :], scalar=omega_sb[:, g, t : t + 1],
+                out=y_sb[g, h][:, t0 + a, :], in0=y_sb[g, h][:, t0 + a, :], scalar=omega_sb[:, g, t0 + a : t0 + a + 1],
                 in1=rate_sb[pair][:, a, h * HALF : (h + 1) * HALF], op0=ALU.mult, op1=ALU.mult,
             )
 
-        def store_y(pair, h):
-            g, t0 = pair // 2, 2 * (pair % 2)
+        def store_y(pair, h, a_lo=0, a_hi=2):
+            g, t0 = tiles_of(pair)
             nc.sync.dma_start(
-                out=out_rows[g][:, t0 : t0 + 2, h * HALF : (h + 1) * HALF], in_=y_sb[g, h][:, t0 : t0 + 2, :]
+                out=out_rows[g][:, t0 + a_lo : t0 + a_hi, h * HALF : (h + 1) * HALF],
+                in_=y_sb[g, h][:, t0 + a_lo : t0 + a_hi, :],
             )
 
-        def y_interleave(g, lo, hi, on_vector):
+        def y_interleave(g, lo, hi, copy):
             h = lo // HALF
-            yg = work.tile([P, hi - lo, PACK], BF16, name="yg", tag="yg", bufs=3, align_bytes=64)
-            interleave(on_vector, yg[:], y_sb[g, h][:, :, lo - h * HALF : hi - h * HALF])
-            y_grouped[g, lo] = yg
+            y_bf[g, lo] = work.tile([P, hi - lo, PACK], BF16, name="yg", tag="yg", bufs=3, align_bytes=64)
+            interleave(copy, y_bf[g, lo][:], y_sb[g, h][:, :, lo - h * HALF : hi - h * HALF])
 
         def y_quantise(g, lo, hi):
-            nc.vector.quantize_mx(
-                out=y_codes[g][:, lo:hi].bitcast(FP8X4), scales=y_scales[g][:, lo:hi],
-                in_=y_grouped[g, lo][:].rearrange("p n t -> p (n t)"),
-            )
-
-        def store_codes(g, lo, hi):
+            quantise(y_codes[g][:, lo:hi], y_scales[g][:, lo:hi], y_bf[g, lo][:])
             nc.sync.dma_start(
                 out=out_1[g].rearrange("p n t -> p (n t)").bitcast(I32)[:, lo:hi], in_=y_codes[g][:, lo:hi].bitcast(I32)
             )
 
         def store_scales(g, queues):
-            for quad in range(4):
-                queues[quad].dma_start(
+            for quad in range(QUADRANTS):
+                queues[quad % len(queues)].dma_start(
                     out=out_2[g, 4 * quad : 4 * quad + 4, :].bitcast(I32),
                     in_=y_scales[g][32 * quad : 32 * quad + 4, :].bitcast(I32),
                 )
 
-        turn(z_bank, z_sb, "zb", 0)
-        turn(z_bank, z_sb, "zb", 1)
-        turn(zdot_bank, zdot_sb, "zdb", 0)
-        tanh_step(0)
-        v_interleave(0, 0, True)
-        h_step(0)
-        v_interleave(0, 1, True)
-        v_quantise(0, 0)
+        on_vector, on_scalar = nc.vector.tensor_copy, nc.scalar.copy
 
-        for s in range(CHUNKS):
-            done, phase = divmod(s - PASSES, PASSES)
-            busy = done >= 0
-            if busy and phase == 1:
-                add_bias(done, 0, 1)
-                add_bias(done, 1, 1)
-            if s + 2 < CHUNKS:
-                turn(z_bank, z_sb, "zb", s + 2)
-            if s >= 1:
-                multiply(s - 1, 0)
-            if s + 1 < CHUNKS:
-                turn(zdot_bank, zdot_sb, "zdb", s + 1)
-            if s >= 1:
-                multiply(s - 1, 1)
-
+        def scalar_steps(s):
             square_step(s)
             if s + 1 < CHUNKS:
                 tanh_step(s + 1)
             slope_step(s)
-            if s + 1 < PASSES:
-                v_interleave(s + 1, 1, False)
-            if s == 8 or s == 10:
-                y_interleave(0, (s - 8) // 2 * HALF, (s - 6) // 2 * HALF, False)
 
-            if s < PASSES:
+
+        turn_z(0)
+        turn_z(1)
+        turn_zdot(0)
+        tanh_step(0)
+        v_interleave(0, 0, on_vector)
+        h_step(0, 0, COLS, nc.vector)
+        v_quantise(0, 0)
+        v_interleave(0, 1, on_vector)
+        for s in range(PASSES):
+            turn_z(s + 2)
+            if s > 0:
+                multiply(s - 1, 0)
+                multiply(s - 1, 1)
+            turn_zdot(s + 1)
+            scalar_steps(s)
+            if s == 1:
+                v_interleave(s, 1, on_scalar)
+            if s == 2:
+                v_interleave(s, 1, on_scalar, 0, QUARTER)
+            h_step(s + 1, 0, P, nc.gpsimd)
+            hdot_step(s)
+            if s == 0:
                 v_quantise(s, 1)
             if s + 1 < PASSES:
-                v_interleave(s + 1, 0, True)
-            hdot_step(s)
-            if s + 1 < CHUNKS:
-                h_step(s + 1)
-            if busy and phase == 0:
-                add_bias(done, 0, 0)
-                add_bias(done, 1, 0)
-            if s == 9:
-                y_quantise(0, 0, HALF)
-                store_codes(0, 0, HALF)
-            if busy and phase >= 1:
-                weigh(done, 0, phase - 1)
-                if s + 1 < CHUNKS:
-                    weigh(done, 1, phase - 1)
-                    store_y(done, phase - 1)
-            quantise_step(s)
+                v_interleave(s + 1, 0, on_vector)
+            else:
+                v_interleave(s, 1, on_vector, QUARTER, HALF)
+            h_step(s + 1, P, COLS, nc.vector)
             if s + 1 < PASSES:
                 v_quantise(s + 1, 0)
+            if s > 0:
+                v_quantise(s, 1)
+            quantise_step(s)
+        turn_z(PASSES + 2)
+        turn_zdot(PASSES + 1)
 
-        weigh(PAIRS - 2, 1, 1)
-        store_y(PAIRS - 2, 1)
-        y_quantise(0, HALF, N)
-        store_codes(0, HALF, N)
-        store_scales(0, [nc.sync] * 4)
+        first_group_done = 3 * PASSES
+        for s in range(PASSES, CHUNKS):
+            done, c = s // PASSES - 1, s % PASSES
+            last_chunk = s + 1 == CHUNKS
+            if c == 1:
+                add_bias(done, 0, 1)
+                add_bias(done, 1, 1)
+            multiply(s - 1, 0)
+            scalar_steps(s)
+            if s == first_group_done:
+                y_interleave(0, 0, HALF, on_scalar)
+            if last_chunk:
+                y_interleave(0, HALF, N, on_scalar)
+            else:
+                multiply(s - 1, 1)
+            if s + 3 < CHUNKS:
+                turn_z(s + 3)
+            if not last_chunk:
+                h_step(s + 1, 0, COLS if c < 2 else P, nc.gpsimd)
+            hdot_step(s)
+            if s + 2 < CHUNKS:
+                turn_zdot(s + 2)
+            if c == 0:
+                add_bias(done, 0, 0)
+                add_bias(done, 1, 0)
+            if s == first_group_done:
+                y_quantise(0, 0, HALF)
+            if c > 0:
+                weigh(done, 0, c - 1)
+            if c > 0 and not last_chunk:
+                weigh(done, 1, c - 1)
+                store_y(done, c - 1)
+            if c == 2 and not last_chunk:
+                h_step(s + 1, P, COLS, nc.vector)
+            quantise_step(s)
+
         last = PAIRS - 1
+        weigh(last - 1, 1, 1)
+        store_y(last - 1, 1)
+        y_quantise(0, HALF, N)
+        store_scales(0, [nc.sync])
         multiply(CHUNKS - 1, 0)
+        multiply(CHUNKS - 2, 1)
         multiply(CHUNKS - 1, 1)
         for h in range(HALVES):
             add_bias(last, 0, h)
             add_bias(last, 1, h)
-            weigh(last, 0, h)
-            weigh(last, 1, h)
-            store_y(last, h)
+            for a in range(2):
+                weigh(last, a, h)
+                store_y(last, h, a, a + 1)
             if h == 0:
-                y_interleave(1, 0, HALF, False)
-        y_interleave(1, 768, N, False)
+                y_interleave(1, 0, HALF, on_scalar)
+        y_interleave(1, HALF + QUARTER, N, on_scalar)
+        y_interleave(1, HALF, HALF + QUARTER, on_vector)
         y_quantise(1, 0, HALF)
-        store_codes(1, 0, HALF)
-        y_interleave(1, HALF, 768, True)
-        y_quantise(1, HALF, 768)
-        y_quantise(1, 768, N)
-        store_codes(1, HALF, N)
-        store_scales(1, [nc.scalar, nc.sync, nc.scalar, nc.sync])
+        y_quantise(1, HALF, HALF + QUARTER)
+        y_quantise(1, HALF + QUARTER, N)
+        store_scales(1, [nc.scalar, nc.sync])

from contextlib import ExitStack

import concourse.mybir as mybir
from concourse.masks import make_identity

M, K, N = 1024, 1536, 1024
FLOPS = 2 * 2 * M * K * N

F32 = mybir.dt.float32
BF16 = mybir.dt.bfloat16
I32 = mybir.dt.int32
U32 = mybir.dt.uint32
U8 = mybir.dt.uint8
FP8X4 = mybir.dt.float8_e4m3fn_x4
FP4X4 = mybir.dt.float4_e2m1fn_x4
ACT = mybir.ActivationFunctionType
ALU = mybir.AluOpType

P = 128
PACK = 4
K_PASS = P * PACK
PASSES = K // K_PASS
HALF = 512
HALVES = N // HALF
GROUPS = M // K_PASS
PAIRS = 2 * GROUPS
CHUNKS = PAIRS * PASSES
COLS = 2 * P
QUADRANTS = 4
RUN = 4
QUARTER = HALF // 2


def tile_gauss_newton_curvature_product_g5_kernel(
    tc, z, zdot, gain, v, w_words, w_scales, vb, rate, omega, out_0, out_1, out_2
):
    nc = tc.nc
    with ExitStack() as ctx:
        keep = ctx.enter_context(tc.tile_pool(name="keep", bufs=1))
        work = ctx.enter_context(tc.tile_pool(name="work", bufs=2))
        psum = ctx.enter_context(tc.psum_pool(name="psum", bufs=1))
        ctx.enter_context(tc.manual_schedule())

        z_rows = z.rearrange("(g p t) k -> g p t k", p=P, t=PACK)
        zdot_rows = zdot.rearrange("(g p t) k -> g p t k", p=P, t=PACK)
        rate_rows = rate.rearrange("(g p t) n -> g p t n", p=P, t=PACK)
        out_rows = out_0.rearrange("(g p t) n -> g p t n", p=P, t=PACK)
        v_rows = v.rearrange("(c p t) n -> c p t n", p=P, t=PACK)

        def tiles_of(pair):
            return pair // 2, 2 * (pair % 2)

        ident = keep.tile([P, P], F32, name="ident")
        make_identity(nc, ident[:])
        w_sc = keep.tile([P, PASSES, N], U8, name="w_sc", align_bytes=64)
        nc.gpsimd.memset(w_sc[:].rearrange("p c n -> p (c n)").bitcast(I32), 0)

        gain_bf = keep.tile([P, PASSES, PACK], BF16, name="gain_bf")
        nc.scalar.dma_start(out=gain_bf[:], in_=gain.rearrange("(c p t) -> p c t", p=P, t=PACK))

        z_sb, zdot_sb, v_raw, w_sb, rate_sb = {}, {}, {}, {}, {}

        def load_rows(chunks, rows, label, pair, c_lo, c_hi):
            g, t0 = tiles_of(pair)
            raw = keep.tile([P, 2, (c_hi - c_lo) * K_PASS], BF16, name="%s_%d_%d" % (label, pair, c_lo))
            nc.sync.dma_start(out=raw[:], in_=rows[g][:, t0 : t0 + 2, c_lo * K_PASS : c_hi * K_PASS])
            for c in range(c_lo, c_hi):
                chunks[PASSES * pair + c] = raw[:, :, (c - c_lo) * K_PASS : (c - c_lo + 1) * K_PASS]

        def load_z(pair, c_lo=0, c_hi=PASSES):
            load_rows(z_sb, z_rows, "z", pair, c_lo, c_hi)

        def load_zdot(pair, c_lo=0, c_hi=PASSES):
            load_rows(zdot_sb, zdot_rows, "zd", pair, c_lo, c_hi)

        def load_v(c, h_lo=0, h_hi=HALVES):
            raw = keep.tile([P, PACK, (h_hi - h_lo) * HALF], BF16, name="v_raw_%d_%d" % (c, h_lo))
            nc.sync.dma_start(out=raw[:], in_=v_rows[c][:, :, h_lo * HALF : h_hi * HALF])
            for h in range(h_lo, h_hi):
                v_raw[c, h] = raw[:, :, (h - h_lo) * HALF : (h - h_lo + 1) * HALF]

        def load_w(c_lo, c_hi):
            raw = keep.tile([P, c_hi - c_lo, 2 * N], U8, name="w_%d" % c_lo, align_bytes=64)
            nc.sync.dma_start(out=raw[:].bitcast(I32), in_=w_words[c_lo:c_hi].rearrange("c p b -> p c b").bitcast(I32))
            for c in range(c_lo, c_hi):
                w_sb[c] = raw[:, c - c_lo, :]

        def load_rate(pair):
            g, t0 = tiles_of(pair)
            raw = keep.tile([P, 2, N], BF16, name="rate_%d" % pair)
            nc.sync.dma_start(out=raw[:], in_=rate_rows[g][:, t0 : t0 + 2, :])
            rate_sb[pair] = raw

        load_z(0, 0, 1)
        load_v(0, 0, 1)
        load_z(0, 1, PASSES)
        load_zdot(0, 0, 1)
        load_v(0, 1, HALVES)
        load_v(1)
        load_zdot(0, 1, PASSES)
        load_w(0, 1)
        for quad in range(QUADRANTS):
            nc.sync.dma_start(
                out=w_sc[32 * quad : 32 * quad + 4, :, :].bitcast(I32),
                in_=w_scales[:, 4 * quad : 4 * quad + 4, :].rearrange("c r n -> r c n").bitcast(I32),
            )
        load_z(1, 0, 1)
        load_v(2)
        load_w(1, PASSES)
        load_z(1, 1, PASSES)
        load_zdot(1)
        vb_sb = keep.tile([P, N], BF16, name="vb_sb")
        nc.sync.dma_start(out=vb_sb[:], in_=vb.partition_broadcast(P))
        load_z(2)
        omega_sb = keep.tile([P, GROUPS, PACK], BF16, name="omega_sb")
        nc.sync.dma_start(out=omega_sb[:], in_=omega.rearrange("(g p t) -> p g t", p=P, t=PACK))
        load_rate(0)
        load_zdot(2)
        load_z(3)
        load_rate(1)
        load_zdot(3)
        load_rate(2)
        load_rate(3)

        gain_f = keep.tile([P, PASSES, PACK], F32, name="gain_f")
        neg_gain_f = keep.tile([P, PASSES, PACK], F32, name="neg_gain_f")
        nc.vector.tensor_copy(out=gain_f[:], in_=gain_bf[:])
        nc.vector.tensor_scalar(out=neg_gain_f[:], in0=gain_bf[:], scalar1=-1.0, scalar2=None, op0=ALU.mult)
        gain_row = keep.tile([P, PASSES, COLS, PACK], BF16, name="gain_row")
        nc.vector.tensor_copy(
            out=gain_row[:], in_=gain_bf[:].rearrange("p c (m t) -> p c m t", m=1).to_broadcast([P, PASSES, COLS, PACK])
        )

        z_bank, zdot_bank, tanh_z, tanh_sq, slope, h_bf, hdot_bf, codes, scales = {}, {}, {}, {}, {}, {}, {}, {}, {}

        def turn(banks, chunks, label, s):
            bank = psum.tile([P, 2, COLS], F32, name=label, tag=label, bufs=2)
            for u in range(2):
                for a in range(2):
                    words = chunks[s][:, a, :].bitcast(F32)
                    nc.tensor.transpose(bank[:, u, a * P : (a + 1) * P], words[:, u : 2 * P : 2], ident[:])
            banks[s] = bank

        def turn_z(s):
            turn(z_bank, z_sb, "zb", s)

        def turn_zdot(s):
            turn(zdot_bank, zdot_sb, "zdb", s)

        def tanh_step(s):
            tanh_z[s] = work.tile([P, 2, 2 * COLS], F32, name="th", tag="th", bufs=3)
            nc.scalar.activation(out=tanh_z[s][:], in_=z_bank[s][:].bitcast(BF16), func=ACT.Tanh)

        def square_step(s):
            tanh_sq[s] = work.tile([P, PACK, COLS], F32, name="sq", tag="sq", bufs=2)
            nc.scalar.activation(
                out=tanh_sq[s][:].rearrange("p (u e) m -> p u e m", e=2),
                in_=tanh_z[s][:].rearrange("p u (m e) -> p u e m", e=2),
                func=ACT.Square,
            )

        def slope_step(s):
            c = s % PASSES
            slope[s] = work.tile([P, PACK, COLS], F32, name="sl", tag="sl", bufs=3)
            for t in range(PACK):
                nc.scalar.activation(
                    out=slope[s][:, t, :], in_=tanh_sq[s][:, t, :], func=ACT.Identity,
                    scale=neg_gain_f[:, c, t : t + 1], bias=gain_f[:, c, t : t + 1],
                )

        def h_step(s, lo, hi, engine):
            if lo == 0:
                h_bf[s] = work.tile([P, COLS, PACK], BF16, name="hb", tag="hb", bufs=2, align_bytes=64)
            engine.tensor_tensor(
                out=h_bf[s][:, lo:hi, :].rearrange("p m (u e) -> p m u e", e=2),
                in0=tanh_z[s][:, :, 2 * lo : 2 * hi].rearrange("p u (m e) -> p m u e", e=2),
                in1=gain_row[:, s % PASSES, lo:hi, :].rearrange("p m (u e) -> p m u e", e=2),
                op=ALU.mult,
            )

        def hdot_step(s):
            hdot_bf[s] = work.tile([P, COLS, PACK], BF16, name="hb", tag="hd", bufs=2, align_bytes=64)
            nc.vector.tensor_tensor(
                out=hdot_bf[s][:].rearrange("p m (u e) -> p m u e", e=2),
                in0=zdot_bank[s][:].bitcast(BF16).rearrange("p u (m e) -> p m u e", e=2),
                in1=slope[s][:].rearrange("p (u e) m -> p m u e", e=2),
                op=ALU.mult,
            )

        def quantise(words, scale_bytes, values):
            nc.vector.quantize_mx(out=words.bitcast(FP8X4), scales=scale_bytes, in_=values.rearrange("p n t -> p (n t)"))

        def quantise_step(s):
            codes[s] = work.tile([P, 2, COLS], U32, name="hc", tag="hc", bufs=3, align_bytes=64)
            scales[s] = work.tile([P, 2, COLS], U8, name="hs", tag="hs", bufs=3, align_bytes=64)
            quantise(codes[s][:, 0, :], scales[s][:, 0, :], h_bf[s][:])
            quantise(codes[s][:, 1, :], scales[s][:, 1, :], hdot_bf[s][:])

        def interleave(copy, out, in_):
            copy(out=out.rearrange("p (q i) t -> p q t i", i=RUN), in_=in_.rearrange("p t (q i) -> p q t i", i=RUN))

        v_bf, v_codes, v_scales, acc = {}, {}, {}, {}

        def v_interleave(c, h, copy, lo=0, hi=HALF):
            if lo == 0:
                v_bf[c, h] = work.tile([P, HALF, PACK], BF16, name="vg", tag="vg", bufs=3, align_bytes=64)
            interleave(copy, v_bf[c, h][:, lo:hi, :], v_raw[c, h][:, :, lo:hi])

        def v_quantise(c, h):
            v_codes[c, h] = keep.tile([P, HALF], U32, name="vc_%d_%d" % (c, h), align_bytes=64)
            v_scales[c, h] = keep.tile([P, HALF], U8, name="vs_%d_%d" % (c, h), align_bytes=64)
            quantise(v_codes[c, h][:], v_scales[c, h][:], v_bf[c, h][:])

        def multiply(s, h):
            pair, c = divmod(s, PASSES)
            for a in range(2):
                if c == 0:
                    acc[pair, a, h] = psum.tile([P, HALF], F32, name="acc", tag="acc_%d_%d" % (a, h), bufs=1)
                tile_cols = slice(a * P, (a + 1) * P)
                nc.tensor.matmul_mx(
                    out=acc[pair, a, h][:],
                    lhsT=codes[s][:, 0, tile_cols].bitcast(FP8X4), lhsT_scale=scales[s][:, 0, tile_cols],
                    rhs=v_codes[c, h][:].bitcast(FP8X4), rhs_scale=v_scales[c, h][:],
                    start=(c == 0), stop=False,
                )
                nc.tensor.matmul_mx(
                    out=acc[pair, a, h][:],
                    lhsT=codes[s][:, 1, tile_cols].bitcast(FP8X4), lhsT_scale=scales[s][:, 1, tile_cols],
                    rhs=w_sb[c][:, 2 * h * HALF : 2 * (h + 1) * HALF].bitcast(FP4X4),
                    rhs_scale=w_sc[:, c, h * HALF : (h + 1) * HALF],
                    start=False, stop=(c == PASSES - 1),
                )

        y_sb, y_bf, y_codes, y_scales = {}, {}, {}, {}
        for g in range(GROUPS):
            for h in range(HALVES):
                y_sb[g, h] = keep.tile([P, PACK, HALF], F32, name="y_%d_%d" % (g, h))
            y_codes[g] = keep.tile([P, N], U32, name="y_codes_%d" % g, align_bytes=64)
            y_scales[g] = keep.tile([P, N], U8, name="y_scales_%d" % g, align_bytes=64)

        def add_bias(pair, a, h):
            g, t0 = tiles_of(pair)
            nc.vector.tensor_tensor(
                out=y_sb[g, h][:, t0 + a, :], in0=acc[pair, a, h][:], in1=vb_sb[:, h * HALF : (h + 1) * HALF], op=ALU.add
            )

        def weigh(pair, a, h):
            g, t0 = tiles_of(pair)
            nc.vector.scalar_tensor_tensor(
                out=y_sb[g, h][:, t0 + a, :], in0=y_sb[g, h][:, t0 + a, :], scalar=omega_sb[:, g, t0 + a : t0 + a + 1],
                in1=rate_sb[pair][:, a, h * HALF : (h + 1) * HALF], op0=ALU.mult, op1=ALU.mult,
            )

        def store_y(pair, h, a_lo=0, a_hi=2):
            g, t0 = tiles_of(pair)
            nc.sync.dma_start(
                out=out_rows[g][:, t0 + a_lo : t0 + a_hi, h * HALF : (h + 1) * HALF],
                in_=y_sb[g, h][:, t0 + a_lo : t0 + a_hi, :],
            )

        def y_interleave(g, lo, hi, copy):
            h = lo // HALF
            y_bf[g, lo] = work.tile([P, hi - lo, PACK], BF16, name="yg", tag="yg", bufs=3, align_bytes=64)
            interleave(copy, y_bf[g, lo][:], y_sb[g, h][:, :, lo - h * HALF : hi - h * HALF])

        def y_quantise(g, lo, hi):
            quantise(y_codes[g][:, lo:hi], y_scales[g][:, lo:hi], y_bf[g, lo][:])
            nc.sync.dma_start(
                out=out_1[g].rearrange("p n t -> p (n t)").bitcast(I32)[:, lo:hi], in_=y_codes[g][:, lo:hi].bitcast(I32)
            )

        def store_scales(g, queues):
            for quad in range(QUADRANTS):
                queues[quad % len(queues)].dma_start(
                    out=out_2[g, 4 * quad : 4 * quad + 4, :].bitcast(I32),
                    in_=y_scales[g][32 * quad : 32 * quad + 4, :].bitcast(I32),
                )

        on_vector, on_scalar = nc.vector.tensor_copy, nc.scalar.copy

        def scalar_steps(s):
            square_step(s)
            if s + 1 < CHUNKS:
                tanh_step(s + 1)
            slope_step(s)


        turn_z(0)
        turn_z(1)
        turn_zdot(0)
        tanh_step(0)
        v_interleave(0, 0, on_vector)
        h_step(0, 0, COLS, nc.vector)
        v_quantise(0, 0)
        v_interleave(0, 1, on_vector)
        for s in range(PASSES):
            turn_z(s + 2)
            if s > 0:
                multiply(s - 1, 0)
                multiply(s - 1, 1)
            turn_zdot(s + 1)
            scalar_steps(s)
            if s == 1:
                v_interleave(s, 1, on_scalar)
            if s == 2:
                v_interleave(s, 1, on_scalar, 0, QUARTER)
            h_step(s + 1, 0, P, nc.gpsimd)
            hdot_step(s)
            if s == 0:
                v_quantise(s, 1)
            if s + 1 < PASSES:
                v_interleave(s + 1, 0, on_vector)
            else:
                v_interleave(s, 1, on_vector, QUARTER, HALF)
            h_step(s + 1, P, COLS, nc.vector)
            if s + 1 < PASSES:
                v_quantise(s + 1, 0)
            if s > 0:
                v_quantise(s, 1)
            quantise_step(s)
        turn_z(PASSES + 2)
        turn_zdot(PASSES + 1)

        first_group_done = 3 * PASSES
        for s in range(PASSES, CHUNKS):
            done, c = s // PASSES - 1, s % PASSES
            last_chunk = s + 1 == CHUNKS
            if c == 1:
                add_bias(done, 0, 1)
                add_bias(done, 1, 1)
            multiply(s - 1, 0)
            scalar_steps(s)
            if s == first_group_done:
                y_interleave(0, 0, HALF, on_scalar)
            if last_chunk:
                y_interleave(0, HALF, N, on_scalar)
            else:
                multiply(s - 1, 1)
            if s + 3 < CHUNKS:
                turn_z(s + 3)
            if not last_chunk:
                h_step(s + 1, 0, COLS if c < 2 else P, nc.gpsimd)
            hdot_step(s)
            if s + 2 < CHUNKS:
                turn_zdot(s + 2)
            if c == 0:
                add_bias(done, 0, 0)
                add_bias(done, 1, 0)
            if s == first_group_done:
                y_quantise(0, 0, HALF)
            if c > 0:
                weigh(done, 0, c - 1)
            if c > 0 and not last_chunk:
                weigh(done, 1, c - 1)
                store_y(done, c - 1)
            if c == 2 and not last_chunk:
                h_step(s + 1, P, COLS, nc.vector)
            quantise_step(s)

        last = PAIRS - 1
        weigh(last - 1, 1, 1)
        store_y(last - 1, 1)
        y_quantise(0, HALF, N)
        store_scales(0, [nc.sync])
        multiply(CHUNKS - 1, 0)
        multiply(CHUNKS - 2, 1)
        multiply(CHUNKS - 1, 1)
        for h in range(HALVES):
            add_bias(last, 0, h)
            add_bias(last, 1, h)
            for a in range(2):
                weigh(last, a, h)
                store_y(last, h, a, a + 1)
            if h == 0:
                y_interleave(1, 0, HALF, on_scalar)
        y_interleave(1, HALF + QUARTER, N, on_scalar)
        y_interleave(1, HALF, HALF + QUARTER, on_vector)
        y_quantise(1, 0, HALF)
        y_quantise(1, HALF, HALF + QUARTER)
        y_quantise(1, HALF + QUARTER, N)
        store_scales(1, [nc.scalar, nc.sync])
